import numpy as np
import ml_dtypes


def mxq(x, axis, fmt="e4m3"):
    dtype, down = {"e4m3": (ml_dtypes.float8_e4m3fn, 7), "e5m2": (ml_dtypes.float8_e5m2, 14)}[fmt]
    v = np.moveaxis(np.asarray(x, np.float32).astype(ml_dtypes.bfloat16).astype(np.float64), axis, -1)
    blocks = v.reshape(v.shape[:-1] + (-1, 32))
    amax = np.abs(blocks).max(-1, keepdims=True)
    byte = np.maximum(np.where(amax > 0, np.frexp(amax)[1] - 1 + 127, 0) - down, 1)
    scale = np.exp2(byte - 127.0)
    codes = (blocks / scale).astype(np.float32).astype(dtype).astype(np.float64)
    return np.moveaxis((codes * scale).reshape(v.shape), -1, axis)


WIDE = False


def mx_kscale(k):
    if not WIDE:
        return np.ones(k)
    levels = np.array([10, -10, 5, -5, 0])
    if k % 512:
        return np.exp2(np.random.permutation(np.resize(levels, k // 32))).repeat(32)
    a = np.empty((k // 512, 16))
    for p in range(k // 512):
        a[p, :8] = np.random.permutation(np.resize(levels, 8))
        for g in range(8):
            far = levels[np.abs(levels - a[p, g]) >= 10]
            a[p, g + 8] = far[np.random.randint(len(far))]
    return np.exp2(a.ravel()).repeat(32)


BF16 = ml_dtypes.bfloat16


def bf(x):
    return np.asarray(x, np.float32).astype(BF16)


def f64(x):
    return np.asarray(x).astype(np.float64)


E2M1 = np.array([0.0, 0.5, 1.0, 1.5, 2.0, 3.0, 4.0, 6.0, -0.0, -0.5, -1.0, -1.5, -2.0, -3.0, -4.0, -6.0])


def pack_weight(w, fmt):
    k, n = w.shape
    w = f64(bf(w)).reshape(k // 32, 32, n)
    amax = np.abs(w).max(1)
    if fmt == "e4m3":
        byte = np.frexp(amax)[1] - 1 + 127 - 7
    else:
        mant, ex = np.frexp(amax / 6.0)
        byte = np.where(mant > 0.5, ex, ex - 1) + 127
    byte = np.clip(np.where(amax > 0, byte, 1), 1, 254)
    scaled = (w * np.exp2(127.0 - byte)[:, None, :]).reshape(k, n).astype(np.float32)
    by_word = np.ascontiguousarray(scaled.reshape(k // 512, 128, 4, n).transpose(0, 1, 3, 2))
    if fmt == "e4m3":
        words = by_word.astype(ml_dtypes.float8_e4m3fn).view(np.uint8)
    else:
        c = by_word.astype(ml_dtypes.float4_e2m1fn).view(np.uint8) & 0xF
        words = c[..., 0::2] | (c[..., 1::2] << 4)
    return np.ascontiguousarray(words), np.ascontiguousarray(byte.astype(np.uint8).reshape(k // 512, 16, n))


def unpack_weight(words, scales, fmt):
    g, p, n, _ = words.shape
    if fmt == "e4m3":
        vals = np.ascontiguousarray(words).view(ml_dtypes.float8_e4m3fn).astype(np.float64)
    else:
        nib = np.empty((g, p, n, 4), np.uint8)
        nib[..., 0::2] = words & 0xF
        nib[..., 1::2] = words >> 4
        vals = E2M1[nib]
    vals = vals * np.repeat(np.exp2(scales.astype(np.float64) - 127.0), 8, axis=1)[..., None]
    return vals.transpose(0, 1, 3, 2).reshape(g * 512, n)
def pack4(w):
    words, scales = pack_weight(w, "e2m1")
    return words.reshape(words.shape[0], 128, -1), scales


def unpack4(words, scales):
    return unpack_weight(words.reshape(words.shape[0], 128, -1, 2), scales, "e2m1")


def planes(Y):
    n, m = Y.shape
    b = f64(bf(Y)).reshape(n // 32, 32, m)
    amax = np.abs(b).max(1)
    byte = np.clip(np.where(amax > 0, np.frexp(amax)[1] - 1 + 127 - 7, 1), 1, 254)
    codes = (b * np.exp2(127.0 - byte)[:, None, :]).reshape(n, m).astype(np.float32).astype(ml_dtypes.float8_e4m3fn).view(np.uint8)
    words = codes.reshape(n // 512, 128, 4, m).transpose(0, 1, 3, 2)
    return np.ascontiguousarray(words), np.ascontiguousarray(byte.astype(np.uint8).reshape(n // 512, 16, m))


N, D, M, T = 2048, 512, 1024, 512

LAM = 64.0


def leaf_score(grad, hess):
    return grad * grad / (hess + LAM)


def setup_inputs():
    u, t = mx_kscale(D), mx_kscale(N)
    x = bf(np.random.standard_normal((N, D)) * u)
    p_words, p_scales = pack4(np.random.standard_normal((D, M)) * 2.0 / np.sqrt(D) / u[:, None])
    b = bf(np.random.standard_normal(M) * 0.5)
    w = bf((1.0 + 0.1 * np.random.standard_normal(N)) * t)
    g = bf(np.random.standard_normal((N, T)) * 90.0 / np.sqrt(N) / t[:, None])
    h = bf(np.random.uniform(1.0 / 3.0, 5.0 / 3.0, N) * 48.0 * LAM / N)
    return {"x": x, "p_words": p_words, "p_scales": p_scales, "b": b, "w": w, "g": g, "h": h}


def core(x, p_words, p_scales, b, w, g, h):
    w64, g64, h64 = f64(w), f64(g), f64(h)
    z = (mxq(f64(x), 1, "e4m3") @ unpack4(p_words, p_scales)) + f64(b)[None, :]
    s = np.tanh(z / 2.0)
    d = mxq((s * w64[:, None]).T, 1, "e4m3") @ mxq(g64, 0, "e4m3")
    gt = np.sum(w64[:, None] * g64, axis=0)
    hd = np.sum(s * h64[:, None], axis=0)
    ht = np.sum(h64)
    GL = (gt[None, :] - d) / 2.0
    GR = (gt[None, :] + d) / 2.0
    HL = ((ht - hd) / 2.0)[:, None]
    HR = ((ht + hd) / 2.0)[:, None]
    return 0.5 * (leaf_score(GL, HL) + leaf_score(GR, HR) - leaf_score(gt[None, :], ht))


def reference(x, p_words, p_scales, b, w, g, h):
    R_out = core(x, p_words, p_scales, b, w, g, h)
    words, scales = planes(R_out.T)
    return R_out, words, scales

@@ -1,0 +1,446 @@
+from contextlib import ExitStack
+
+import concourse.mybir as mybir
+from concourse.masks import make_identity
+
+N, D, M, T = 2048, 512, 1024, 512
+FLOPS = 2 * N * D * M + 2 * N * M * T
+
+F32 = mybir.dt.float32
+BF16 = mybir.dt.bfloat16
+U32 = mybir.dt.uint32
+I32 = mybir.dt.int32
+U8 = mybir.dt.uint8
+FP8X4 = mybir.dt.float8_e4m3fn_x4
+FP4X4 = mybir.dt.float4_e2m1fn_x4
+ACT = mybir.ActivationFunctionType
+ALU = mybir.AluOpType
+AX = mybir.AxisListType
+
+P = 128
+NG = N // 512
+MT = M // P
+LAM = 64.0
+HD_ON_V = (0, 2)
+
+
+def tile_obliquesoftsplitgaintable_x2_kernel(tc, x, p_words, p_scales, b, w, g, h, out_0, out_1, out_2):
+    nc = tc.nc
+    with ExitStack() as ctx:
+        keep = ctx.enter_context(tc.tile_pool(name="keep", bufs=1))
+        four = ctx.enter_context(tc.tile_pool(name="four", bufs=4))
+        three = ctx.enter_context(tc.tile_pool(name="three", bufs=3))
+        two = ctx.enter_context(tc.tile_pool(name="two", bufs=2))
+        ps3 = ctx.enter_context(tc.psum_pool(name="ps3", bufs=3))
+        ps1 = ctx.enter_context(tc.psum_pool(name="ps1", bufs=1))
+        ctx.enter_context(tc.manual_schedule())
+
+        x_raw, g_raw = [], []
+        for G in range(NG):
+            xr = four.tile([P, 4, D], BF16, name="x_raw", align_bytes=64)
+            x_raw.append(xr)
+        for G in range(NG):
+            gr = four.tile([P, 4, T], BF16, name="g_raw", align_bytes=64)
+            g_raw.append(gr)
+        pw = keep.tile([P, 2 * M], U8, name="pw", align_bytes=64)
+        psc = keep.tile([P, M], U8, name="psc", align_bytes=64)
+        w_sb = keep.tile([P, NG, 4], BF16, name="w_sb")
+        h_sb = keep.tile([P, NG, 4], BF16, name="h_sb")
+        b_rows = keep.tile([P, P], BF16, name="b_rows", align_bytes=64)
+
+        nc.vector.memset(psc[:].bitcast(I32), 0)
+        nc.vector.memset(b_rows[:], 0.0)
+
+        def load_x(G):
+            nc.sync.dma_start(out=x_raw[G][:], in_=x[512 * G : 512 * (G + 1), :].rearrange("(p j) k -> p j k", j=4))
+
+        load_x(0)
+        nc.sync.dma_start(out=pw[:].bitcast(I32), in_=p_words[0].bitcast(I32))
+        for G in range(1, NG):
+            load_x(G)
+        for G in range(NG):
+            nc.sync.dma_start(out=g_raw[G][:], in_=g[512 * G : 512 * (G + 1), :].rearrange("(p j) t -> p j t", j=4))
+        nc.scalar.dma_start(out=h_sb[:], in_=h.rearrange("(g p j) -> p g j", p=P, j=4))
+        nc.scalar.dma_start(out=w_sb[:], in_=w.rearrange("(g p j) -> p g j", p=P, j=4))
+        nc.scalar.dma_start(out=b_rows[0:MT, :], in_=b.rearrange("(i c) -> i c", c=P))
+        for r in range(4):
+            nc.scalar.dma_start(out=psc[r:P:32, :].bitcast(I32), in_=p_scales[0, r:16:4, :].bitcast(I32))
+
+        ident_f = keep.tile([P, P], F32, name="ident_f", align_bytes=64)
+        ident_b = keep.tile([P, P], BF16, name="ident_b", align_bytes=64)
+        make_identity(nc, ident_f[:])
+        make_identity(nc, ident_b[:])
+        neg_half = keep.tile([P, 1], F32, name="neg_half")
+
+        xc = [keep.tile([P, 512], U32, name="xc%d" % G, align_bytes=64) for G in range(NG)]
+        xs = [keep.tile([P, 512], U8, name="xs%d" % G, align_bytes=64) for G in range(NG)]
+        gc = [keep.tile([P, T], U32, name="gc%d" % G, align_bytes=64) for G in range(NG)]
+        gs = [keep.tile([P, T], U8, name="gs%d" % G, align_bytes=64) for G in range(NG)]
+        h_bc = keep.tile([P, NG, 512], BF16, name="h_bc", align_bytes=64)
+        ht4 = keep.tile([P, NG], F32, name="ht4")
+        gt_sb = keep.tile([P, T], F32, name="gt_sb", align_bytes=64)
+        ngt2 = keep.tile([P, T], F32, name="ngt2", align_bytes=64)
+        b_half = keep.tile([P, MT], F32, name="b_half")
+        oc = [keep.tile([P, 256], U32, name="oc%d" % a, align_bytes=64) for a in range(MT // 2)]
+        osc = keep.tile([P, M], U8, name="osc", align_bytes=64)
+
+        def transpose_x(G):
+            words = x_raw[G][:].bitcast(F32)
+            banks = []
+            for a in range(2):
+                bank = ps3.tile([P, 2, 2, P], F32, name="x_ps", tag="tb" if a == 0 else "zb")
+                for jj in range(2):
+                    for u in range(2):
+                        nc.tensor.transpose(bank[:, jj, u, :], words[:, 2 * a + jj, u::2], ident_f[:])
+                banks.append(bank)
+            return banks
+
+        def evac_x(G, banks, engines):
+            xg = three.tile([P, 2048], BF16, name="xg", align_bytes=64)
+            pairs = xg[:].bitcast(F32).rearrange("p (c u) -> p c u", u=2)
+            for a in range(2):
+                dst = pairs[:, 256 * a : 256 * (a + 1), :].rearrange("p (j r) u -> p j r u", j=2)
+                src = banks[a][:].rearrange("p j u r -> p j r u")
+                if engines[a] == "v":
+                    nc.vector.tensor_copy(out=dst, in_=src)
+                else:
+                    nc.scalar.copy(out=dst, in_=src)
+            return xg
+
+        def quant_x(G, xg):
+            nc.vector.quantize_mx(out=xc[G][:].bitcast(FP8X4), scales=xs[G][:], in_=xg[:])
+
+        b_ps = ps1.tile([P, P], BF16, name="pl")
+        nc.tensor.transpose(b_ps[:], b_rows[:], ident_b[:])
+        nc.vector.tensor_scalar(out=b_half[:], in0=b_ps[:, 0:MT], scalar1=0.5, scalar2=0.0, op0=ALU.mult, op1=ALU.add)
+
+        def h_spread(G):
+            hb = ps3.tile([P, 4, P], F32, name="hb", tag="tb")
+            for j in range(4):
+                nc.tensor.matmul(out=hb[:, j, :], lhsT=h_sb[:, G, j : j + 1].to_broadcast([P, P]), rhs=ident_b[:], start=True, stop=True)
+            nc.scalar.activation(out=h_bc[:, G, :], in_=hb[:].rearrange("p j n -> p (j n)"), func=ACT.Copy, accum_out=ht4[:, G : G + 1])
+
+        ht = keep.tile([P, 1], F32, name="ht")
+        ssum = keep.tile([P, 1], F32, name="ssum")
+        two_s = keep.tile([P, 1], F32, name="two_s")
+        r_s = keep.tile([P, 1], F32, name="r_s")
+        nr_s = keep.tile([P, 1], F32, name="nr_s")
+        n2r_s = keep.tile([P, 1], F32, name="n2r_s")
+        c_den = keep.tile([P, 1], F32, name="c_den")
+        c_rec = keep.tile([P, 1], F32, name="c_rec")
+        neg_c = keep.tile([P, 1], F32, name="neg_c")
+
+        def head_constants_1():
+            nc.vector.reduce_sum(out=ht[:], in_=ht4[:], axis=AX.X)
+            nc.gpsimd.tensor_scalar(out=ssum[:], in0=ht[:], scalar1=1.0, scalar2=2.0 * LAM, op0=ALU.mult, op1=ALU.add)
+            nc.gpsimd.tensor_scalar(out=two_s[:], in0=ssum[:], scalar1=2.0, scalar2=0.0, op0=ALU.mult, op1=ALU.add)
+            nc.gpsimd.tensor_scalar(out=c_den[:], in0=ht[:], scalar1=LAM, scalar2=ssum[:], op0=ALU.add, op1=ALU.mult)
+
+        def head_constants_2():
+            nc.vector.reciprocal(out=r_s[:], in_=ssum[:])
+            nc.vector.reciprocal(out=c_rec[:], in_=c_den[:])
+            nc.gpsimd.tensor_scalar(out=nr_s[:], in0=r_s[:], scalar1=-1.0, scalar2=0.0, op0=ALU.mult, op1=ALU.add)
+            nc.gpsimd.tensor_scalar(out=n2r_s[:], in0=r_s[:], scalar1=-2.0, scalar2=0.0, op0=ALU.mult, op1=ALU.add)
+            nc.gpsimd.tensor_scalar(out=neg_c[:], in0=c_rec[:], scalar1=-0.5 * LAM, scalar2=0.0, op0=ALU.mult, op1=ALU.add)
+
+        s_t, q_t, hdp_t, tb_t, d_t, v_t, sq_t, r_t, rb_t, pb_t, pg_t, prod_t, z_t = ({} for k in range(13))
+        qc_t, qs_t, hs_t, den_t, k_t = ({} for k in range(5))
+
+        def live(i):
+            return 0 <= i < MT
+
+        def z_step(i, G):
+            if not live(i):
+                return
+            if G == 0:
+                s_t[i] = three.tile([P, NG, 512], F32, name="s", align_bytes=64)
+                q_t[i] = two.tile([P, NG, P, 4], BF16, name="q", align_bytes=64)
+                hdp_t[i] = three.tile([P, NG], F32, name="hdp")
+            zb = ps3.tile([P, 512], F32, name="zb", tag="zb")
+            nc.tensor.matmul_mx(
+                out=zb[:],
+                lhsT=pw[:, 256 * i : 256 * (i + 1)].bitcast(FP4X4),
+                lhsT_scale=psc[:, P * i : P * (i + 1)],
+                rhs=xc[G][:].bitcast(FP8X4),
+                rhs_scale=xs[G][:],
+                start=True,
+                stop=True,
+            )
+            z_t[i, G] = zb
+
+        def tanh(i, G):
+            if not live(i):
+                return
+            nc.scalar.activation(out=s_t[i][:, G, :], in_=z_t[i, G][:], func=ACT.Tanh, bias=b_half[:, i : i + 1], scale=0.5)
+
+        def t_step(i, G):
+            if not live(i):
+                return
+            tb = ps3.tile([P, 4, P], F32, name="tb", tag="tb")
+            for j in range(4):
+                nc.tensor.transpose(tb[:, j, :], s_t[i][:, G, P * j : P * (j + 1)], ident_f[:])
+            tb_t[i, G] = tb
+
+        def evac(i, G):
+            if not live(i):
+                return
+            nc.vector.tensor_tensor(
+                out=q_t[i][:, G, :, :],
+                in0=tb_t[i, G][:].rearrange("p j m -> p m j"),
+                in1=w_sb[:, G, :].unsqueeze(1).to_broadcast([P, P, 4]),
+                op=ALU.mult,
+            )
+
+        def hd_v(i, G):
+            if not live(i) or G not in HD_ON_V:
+                return
+            junk = two.tile([P, 512], F32, name="junk", align_bytes=64)
+            nc.vector.scalar_tensor_tensor(
+                out=junk[:], in0=s_t[i][:, G, :], scalar=1.0, in1=h_bc[:, G, :], op0=ALU.mult, op1=ALU.mult, accum_out=hdp_t[i][:, G : G + 1]
+            )
+
+        def prod(i, G):
+            if not live(i) or G in HD_ON_V:
+                return
+            pr = three.tile([P, 512], F32, name="prod", align_bytes=64)
+            nc.gpsimd.tensor_tensor(out=pr[:], in0=s_t[i][:, G, :], in1=h_bc[:, G, :], op=ALU.mult)
+            prod_t[i, G] = pr
+
+        def acc(i, G):
+            if not live(i) or G in HD_ON_V:
+                return
+            junk2 = two.tile([P, 512], BF16, name="junk2", align_bytes=64)
+            nc.scalar.activation(out=junk2[:], in_=prod_t[i, G][:], func=ACT.Copy, accum_out=hdp_t[i][:, G : G + 1])
+
+        def chain(i):
+            if not live(i):
+                return
+            hd2 = two.tile([P, 2], F32, name="hd2")
+            hd1 = two.tile([P, 1], F32, name="hd1")
+            hq = two.tile([P, 1], F32, name="hq")
+            hs_t[i] = two.tile([P, 1], F32, name="hs")
+            den_t[i] = two.tile([P, 1], F32, name="den")
+            nc.gpsimd.tensor_tensor(out=hd2[:], in0=hdp_t[i][:, 0:2], in1=hdp_t[i][:, 2:4], op=ALU.add)
+            nc.gpsimd.tensor_tensor(out=hd1[:], in0=hd2[:, 0:1], in1=hd2[:, 1:2], op=ALU.add)
+            nc.gpsimd.tensor_scalar(out=hs_t[i][:], in0=hd1[:], scalar1=nr_s[:], scalar2=0.0, op0=ALU.mult, op1=ALU.add)
+            nc.gpsimd.tensor_tensor(out=hq[:], in0=hd1[:], in1=hd1[:], op=ALU.mult)
+            nc.gpsimd.tensor_scalar(out=den_t[i][:], in0=hq[:], scalar1=n2r_s[:], scalar2=two_s[:], op0=ALU.mult, op1=ALU.add)
+
+        def recip(i):
+            if not live(i):
+                return
+            k_t[i] = two.tile([P, 1], F32, name="kk")
+            nc.vector.reciprocal(out=k_t[i][:], in_=den_t[i][:])
+
+        def quant_q(i):
+            if not live(i):
+                return
+            qc_t[i] = two.tile([P, NG, P], U32, name="qc", align_bytes=64)
+            qs_t[i] = two.tile([P, NG, P], U8, name="qs", align_bytes=64)
+            nc.vector.quantize_mx(
+                out=qc_t[i][:].rearrange("p g m -> p (g m)").bitcast(FP8X4),
+                scales=qs_t[i][:].rearrange("p g m -> p (g m)"),
+                in_=q_t[i][:].rearrange("p g m j -> p (g m j)"),
+            )
+
+        def d_step(i):
+            if not live(i):
+                return
+            if i < MT - 1:
+                d_t[i] = ps1.tile([P, T], F32, name="db")
+            else:
+                d_t[i] = ps3.tile([P, T], F32, name="d_last", tag="zb")
+            for G in range(NG):
+                nc.tensor.matmul_mx(
+                    out=d_t[i][:],
+                    lhsT=qc_t[i][:, G, :].bitcast(FP8X4),
+                    lhsT_scale=qs_t[i][:, G, :],
+                    rhs=gc[G][:].bitcast(FP8X4),
+                    rhs_scale=gs[G][:],
+                    start=(G == 0),
+                    stop=(G == NG - 1),
+                )
+
+        def v_step(i):
+            if not live(i):
+                return
+            v_t[i] = two.tile([P, T], F32, name="v", align_bytes=64)
+            nc.vector.scalar_tensor_tensor(out=v_t[i][:], in0=gt_sb[:], scalar=hs_t[i][:], in1=d_t[i][:], op0=ALU.mult, op1=ALU.add)
+
+        def sq_step(i):
+            if not live(i):
+                return
+            sq_t[i] = two.tile([P, T], F32, name="sq", align_bytes=64)
+            nc.scalar.activation(out=sq_t[i][:], in_=v_t[i][:], func=ACT.Square)
+
+        def r_step(i):
+            if not live(i):
+                return
+            r_t[i] = two.tile([P, T], F32, name="r", align_bytes=64)
+            nc.vector.scalar_tensor_tensor(out=r_t[i][:], in0=sq_t[i][:], scalar=k_t[i][:], in1=ngt2[:], op0=ALU.mult, op1=ALU.add)
+            nc.sync.dma_start(out=out_0[P * i : P * (i + 1), :], in_=r_t[i][:])
+
+        def rb_step(i):
+            if not live(i):
+                return
+            rb_t[i] = two.tile([P, T], BF16, name="rb", align_bytes=64)
+            nc.scalar.copy(out=rb_t[i][:], in_=r_t[i][:])
+
+        def p_step(i):
+            if not live(i):
+                return
+            pb = ps1.tile([P, 2, P], F32, name="pl")
+            words = rb_t[i][:].bitcast(F32)
+            for u in range(2):
+                nc.tensor.transpose(pb[:, u, :], words[:, u::2], ident_f[:])
+            pb_t[i] = pb
+
+        def pg_step(i):
+            if not live(i):
+                return
+            pg_t[i] = two.tile([P, 4 * P], BF16, name="pg", align_bytes=64)
+            nc.scalar.copy(out=pg_t[i][:].bitcast(F32).rearrange("p (m u) -> p m u", u=2), in_=pb_t[i][:].rearrange("p u m -> p m u"))
+
+        def qp_step(i):
+            if not live(i):
+                return
+            o = oc[i // 2]
+            c = P * (i % 2)
+            nc.vector.quantize_mx(out=o[:, c : c + P].bitcast(FP8X4), scales=osc[:, P * i : P * (i + 1)], in_=pg_t[i][:])
+            if i % 2 == 1:
+                nc.sync.dma_start(
+                    out=out_1[0].rearrange("p m t -> p (m t)")[:, 4 * P * (i - 1) : 4 * P * (i + 1)].bitcast(I32), in_=o[:].bitcast(I32)
+                )
+            if i == MT - 1:
+                for Q in range(4):
+                    nc.sync.dma_start(out=out_2[0, 4 * Q : 4 * (Q + 1), :].bitcast(I32), in_=osc[32 * Q : 32 * Q + 4, :].bitcast(I32))
+
+        gg_t = {}
+
+        def ig(G, engine):
+            gg_t[G] = four.tile([P, T, 4], BF16, name="gg", align_bytes=64)
+            src = g_raw[G][:].rearrange("p j t -> p t j")
+            if engine == "g":
+                nc.gpsimd.tensor_scalar(out=gg_t[G][:], in0=src, scalar1=1.0, scalar2=0.0, op0=ALU.mult, op1=ALU.add)
+            elif engine == "s":
+                nc.scalar.copy(out=gg_t[G][:], in_=src)
+            else:
+                nc.vector.tensor_copy(out=gg_t[G][:], in_=src)
+
+        def gq(G):
+            nc.vector.quantize_mx(out=gc[G][:].bitcast(FP8X4), scales=gs[G][:], in_=gg_t[G][:].rearrange("p t j -> p (t j)"))
+
+        def gt_step(G, bank):
+            for j in range(4):
+                nc.tensor.matmul(
+                    out=bank[:], lhsT=w_sb[:, G, j : j + 1].to_broadcast([P, P]), rhs=g_raw[G][:, j, :], start=(G == 0 and j == 0), stop=(G == NG - 1 and j == 3)
+                )
+
+        bk0 = transpose_x(0)
+        xg0 = evac_x(0, bk0, "vs")
+        bk1 = transpose_x(1)
+        quant_x(0, xg0)
+        xg1 = evac_x(1, bk1, "vs")
+        z_step(0, 0)
+        tanh(0, 0)
+        h_spread(0)
+        h_spread(1)
+        quant_x(1, xg1)
+        bk2 = transpose_x(2)
+        xg2 = evac_x(2, bk2, "vs")
+        z_step(0, 1)
+        tanh(0, 1)
+        ig(0, "g")
+        t_step(0, 0)
+        quant_x(2, xg2)
+        evac(0, 0)
+        bk3 = transpose_x(3)
+        xg3 = evac_x(3, bk3, "vs")
+        z_step(0, 2)
+        tanh(0, 2)
+        quant_x(3, xg3)
+        t_step(0, 1)
+        h_spread(2)
+        h_spread(3)
+        z_step(0, 3)
+        tanh(0, 3)
+        head_constants_1()
+        ig(1, "g")
+
+        for i in range(1, MT + 3):
+            z_step(i, 0)
+            tanh(i, 0)
+            z_step(i, 1)
+            tanh(i, 1)
+            if i == 1:
+                ig(2, "g")
+                ig(3, "s")
+                prod(0, 1)
+            if i != MT + 1:
+                chain(i - 2)
+            prod(i - 1, 3)
+            if i < MT:
+                d_step(i - 2)
+            evac(i - 1, 1)
+            hd_v(i - 1, 0)
+            if i != MT:
+                v_step(i - 2)
+                sq_step(i - 2)
+            t_step(i - 1, 2)
+            evac(i - 1, 2)
+            recip(i - 2)
+            if i < MT:
+                hd_v(i - 1, 2)
+            t_step(i - 1, 3)
+            evac(i - 1, 3)
+            if i == MT:
+                hd_v(i - 1, 2)
+            p_step(i - 3)
+            pg_step(i - 3)
+            if i == 1:
+                gt_bank = ps1.tile([P, T], F32, name="pl")
+                gt_step(0, gt_bank)
+                gq(0)
+                gt_step(1, gt_bank)
+            if i > 1:
+                acc(i - 1, 1)
+            if i == 2:
+                nc.vector.scalar_tensor_tensor(out=ngt2[:], in0=gt_bank[:], scalar=neg_c[:], in1=gt_sb[:], op0=ALU.mult, op1=ALU.mult)
+            if i < MT:
+                r_step(i - 2)
+                quant_q(i - 1)
+            elif i == MT:
+                acc(i - 1, 3)
+                chain(i - 1)
+                quant_q(i - 1)
+                d_step(i - 2)
+                v_step(i - 2)
+                sq_step(i - 2)
+                d_step(i - 1)
+                r_step(i - 2)
+            else:
+                r_step(i - 2)
+            z_step(i, 2)
+            tanh(i, 2)
+            z_step(i, 3)
+            tanh(i, 3)
+            if i == 1:
+                acc(0, 1)
+            if i != MT:
+                acc(i - 1, 3)
+            rb_step(i - 2)
+            t_step(i, 0)
+            qp_step(i - 3)
+            if i == 1:
+                gq(1)
+            evac(i, 0)
+            prod(i, 1)
+            if i == 1:
+                gq(2)
+                head_constants_2()
+                gq(3)
+            t_step(i, 1)
+            if i == 1:
+                gt_step(2, gt_bank)
+                gt_step(3, gt_bank)
+                nc.scalar.copy(out=gt_sb[:], in_=gt_bank[:])

@@ -21,7 +21,303 @@ P = 128
 NG = N // 512
 MT = M // P
 LAM = 64.0
-HD_ON_V = (0, 2)
+
+XE = ("vs", "vs", "vs", "vs")
+IG = ("g", "s", "g", "s")
+GSET = {0: (), -1: (0, 1, 2)}
+PLAN = (
+    (('ig', 2), 0),
+    (('k1',), 1),
+    (('xt', 0), 2),
+    (('xe', 0, 0), 3),
+    (('xe', 0, 1), 4),
+    (('xq', 0), 5),
+    (('xt', 1), 6),
+    (('xe', 1, 0), 7),
+    (('xe', 1, 1), 8),
+    (('xq', 1), 9),
+    (('wp', 0), 10),
+    (('we', 0), 11),
+    (('hs', 1), 12),
+    (('wp', 2), 13),
+    (('we', 2), 14),
+    (('z', 0, 1), 15),
+    (('th', 0, 1), 16),
+    (('xt', 2), 17),
+    (('xe', 2, 0), 18),
+    (('xe', 2, 1), 19),
+    (('xq', 2), 20),
+    (('z', 0, 0), 21),
+    (('th', 0, 0), 22),
+    (('hs', 0), 23),
+    (('xt', 3), 24),
+    (('xe', 3, 0), 25),
+    (('xe', 3, 1), 26),
+    (('xq', 3), 27),
+    (('wp', 1), 28),
+    (('we', 1), 29),
+    (('z', 0, 2), 30),
+    (('hs', 3), 31),
+    (('z', 1, 1), 32),
+    (('th', 1, 1), 33),
+    (('gq', 2), 34),
+    (('gm', 1, 1), 35),
+    (('t', 0, 1), 36),
+    (('ev', 0, 1), 37),
+    (('t', 0, 0), 38),
+    (('ev', 0, 0), 39),
+    (('hs', 2), 40),
+    (('hd', 0, 0), 41),
+    (('ig', 0), 42),
+    (('th', 0, 2), 43),
+    (('z', 0, 3), 44),
+    (('th', 0, 3), 45),
+    (('z', 1, 2), 46),
+    (('th', 1, 2), 47),
+    (('gm', 1, 2), 48),
+    (('z', 1, 0), 49),
+    (('th', 1, 0), 50),
+    (('gm', 1, 0), 51),
+    (('t', 0, 3), 52),
+    (('ev', 0, 3), 53),
+    (('z', 1, 3), 54),
+    (('t', 0, 2), 55),
+    (('hd', 0, 1), 56),
+    (('ev', 0, 2), 57),
+    (('gq', 0), 58),
+    (('q', 0), 59),
+    (('ig', 1), 60),
+    (('th', 1, 3), 61),
+    (('hd', 1, 0), 62),
+    (('k2',), 63),
+    (('k3',), 64),
+    (('k4',), 65),
+    (('ch', 0), 66),
+    (('gt', 0), 67),
+    (('gt', 1), 68),
+    (('gq', 1), 69),
+    (('ig', 3), 70),
+    (('gq', 3), 71),
+    (('t', 1, 3), 72),
+    (('ev', 1, 3), 73),
+    (('z', 2, 1), 74),
+    (('th', 2, 1), 75),
+    (('gm', 2, 1), 76),
+    (('rk', 0), 77),
+    (('hd', 1, 1), 78),
+    (('tw', 1, 0, 1), 79),
+    (('ew', 1, 0, 1), 80),
+    (('z', 2, 0), 81),
+    (('th', 2, 0), 82),
+    (('gm', 2, 0), 83),
+    (('hd', 2, 0), 84),
+    (('gt', 2), 85),
+    (('gt', 3), 86),
+    (('gtc',), 87),
+    (('z', 2, 2), 88),
+    (('th', 2, 2), 89),
+    (('gm', 2, 2), 90),
+    (('d', 0, 0), 91),
+    (('d', 0, 1), 92),
+    (('v', 0), 93),
+    (('ch', 1), 94),
+    (('tw', 1, 2), 95),
+    (('ew', 1, 2), 96),
+    (('q', 1), 97),
+    (('z', 2, 3), 98),
+    (('th', 2, 3), 99),
+    (('hd', 2, 1), 100),
+    (('tw', 2, 0, 1), 101),
+    (('ew', 2, 0, 1), 102),
+    (('sq', 0), 103),
+    (('z', 3, 0), 104),
+    (('th', 3, 0), 105),
+    (('gm', 3, 0), 106),
+    (('rk', 1), 107),
+    (('ng',), 108),
+    (('r', 0), 109),
+    (('tw', 2, 2), 110),
+    (('ew', 2, 2), 111),
+    (('t', 2, 3), 112),
+    (('ev', 2, 3), 113),
+    (('z', 3, 1), 114),
+    (('th', 3, 1), 115),
+    (('gm', 3, 1), 116),
+    (('d', 1, 0), 117),
+    (('d', 1, 1), 118),
+    (('v', 1), 119),
+    (('q', 2), 120),
+    (('ch', 2), 121),
+    (('z', 3, 2), 122),
+    (('hd', 3, 0), 123),
+    (('th', 3, 2), 124),
+    (('gm', 3, 2), 125),
+    (('z', 3, 3), 126),
+    (('th', 3, 3), 127),
+    (('hd', 3, 1), 128),
+    (('rb', 0), 129),
+    (('z', 4, 0), 130),
+    (('th', 4, 0), 131),
+    (('gm', 4, 0), 132),
+    (('tw', 3, 0, 1), 133),
+    (('ew', 3, 0, 1), 134),
+    (('d', 2, 0), 135),
+    (('t', 3, 3), 136),
+    (('ev', 3, 3), 137),
+    (('sq', 1), 138),
+    (('r', 1), 139),
+    (('d', 2, 1), 140),
+    (('v', 2), 141),
+    (('rk', 2), 142),
+    (('tw', 3, 2), 143),
+    (('ew', 3, 2), 144),
+    (('p', 0), 145),
+    (('pg', 0), 146),
+    (('z', 4, 1), 147),
+    (('th', 4, 1), 148),
+    (('gm', 4, 1), 149),
+    (('q', 3), 150),
+    (('ch', 3), 151),
+    (('z', 4, 2), 152),
+    (('hd', 4, 0), 153),
+    (('th', 4, 2), 154),
+    (('gm', 4, 2), 155),
+    (('sq', 2), 156),
+    (('r', 2), 157),
+    (('z', 4, 3), 158),
+    (('th', 4, 3), 159),
+    (('hd', 4, 1), 160),
+    (('rb', 1), 161),
+    (('d', 3, 0), 162),
+    (('z', 5, 0), 163),
+    (('th', 5, 0), 164),
+    (('gm', 5, 0), 165),
+    (('tw', 4, 0, 1), 166),
+    (('ew', 4, 0, 1), 167),
+    (('rb', 2), 168),
+    (('t', 4, 3), 169),
+    (('ev', 4, 3), 170),
+    (('rk', 3), 171),
+    (('d', 3, 1), 172),
+    (('v', 3), 173),
+    (('tw', 4, 2), 174),
+    (('ew', 4, 2), 175),
+    (('z', 5, 1), 176),
+    (('th', 5, 1), 177),
+    (('gm', 5, 1), 178),
+    (('q', 4), 179),
+    (('ch', 4), 180),
+    (('z', 5, 2), 181),
+    (('hd', 5, 0), 182),
+    (('th', 5, 2), 183),
+    (('gm', 5, 2), 184),
+    (('sq', 3), 185),
+    (('r', 3), 186),
+    (('p', 1), 187),
+    (('pg', 1), 188),
+    (('z', 5, 3), 189),
+    (('th', 5, 3), 190),
+    (('hd', 5, 1), 191),
+    (('d', 4, 0), 192),
+    (('z', 6, 0), 193),
+    (('th', 6, 0), 194),
+    (('gm', 6, 0), 195),
+    (('tw', 5, 0, 1), 196),
+    (('ew', 5, 0, 1), 197),
+    (('t', 5, 3), 198),
+    (('ev', 5, 3), 199),
+    (('rk', 4), 200),
+    (('rb', 3), 201),
+    (('d', 4, 1), 202),
+    (('v', 4), 203),
+    (('tw', 5, 2), 204),
+    (('ew', 5, 2), 205),
+    (('z', 6, 1), 206),
+    (('th', 6, 1), 207),
+    (('gm', 6, 1), 208),
+    (('q', 5), 209),
+    (('ch', 5), 210),
+    (('z', 6, 2), 211),
+    (('th', 6, 2), 212),
+    (('gm', 6, 2), 213),
+    (('p', 2), 214),
+    (('pg', 2), 215),
+    (('hd', 6, 0), 216),
+    (('sq', 4), 217),
+    (('r', 4), 218),
+    (('z', 6, 3), 219),
+    (('th', 6, 3), 220),
+    (('hd', 6, 1), 221),
+    (('d', 5, 0), 222),
+    (('p', 3), 223),
+    (('pg', 3), 224),
+    (('z', 7, 0), 225),
+    (('th', 7, 0), 226),
+    (('gm', 7, 0), 227),
+    (('tw', 6, 0, 1), 228),
+    (('ew', 6, 0, 1), 229),
+    (('t', 6, 3), 230),
+    (('ev', 6, 3), 231),
+    (('rk', 5), 232),
+    (('rb', 4), 233),
+    (('d', 5, 1), 234),
+    (('v', 5), 235),
+    (('tw', 6, 2), 236),
+    (('ew', 6, 2), 237),
+    (('z', 7, 1), 238),
+    (('th', 7, 1), 239),
+    (('gm', 7, 1), 240),
+    (('qp', 0), 241),
+    (('z', 7, 2), 242),
+    (('q', 6), 243),
+    (('qp', 1), 244),
+    (('hd', 7, 0), 245),
+    (('sq', 5), 246),
+    (('r', 5), 247),
+    (('ch', 6), 248),
+    (('z', 7, 3), 249),
+    (('th', 7, 2), 250),
+    (('gm', 7, 2), 251),
+    (('p', 4), 252),
+    (('pg', 4), 253),
+    (('th', 7, 3), 254),
+    (('hd', 7, 1), 255),
+    (('d', 6, 0), 256),
+    (('tw', 7, 0, 1), 257),
+    (('ew', 7, 0, 1), 258),
+    (('t', 7, 3), 259),
+    (('ev', 7, 3), 260),
+    (('rb', 5), 261),
+    (('d', 6, 1), 262),
+    (('v', 6), 263),
+    (('tw', 7, 2), 264),
+    (('ew', 7, 2), 265),
+    (('q', 7), 266),
+    (('rk', 6), 267),
+    (('sq', 6), 268),
+    (('r', 6), 269),
+    (('ch', 7), 270),
+    (('qp', 2), 271),
+    (('p', 5), 272),
+    (('pg', 5), 273),
+    (('rb', 6), 274),
+    (('d', 7, 0), 275),
+    (('rk', 7), 276),
+    (('qp', 3), 277),
+    (('d', 7, 1), 278),
+    (('v', 7), 279),
+    (('sq', 7), 280),
+    (('r', 7), 281),
+    (('p', 6), 282),
+    (('pg', 6), 283),
+    (('rb', 7), 284),
+    (('qp', 4), 285),
+    (('p', 7), 286),
+    (('pg', 7), 287),
+    (('qp', 5), 288),
+    (('qp', 6), 289),
+    (('qp', 7), 290),
+)
 
 
 def tile_obliquesoftsplitgaintable_x2_kernel(tc, x, p_words, p_scales, b, w, g, h, out_0, out_1, out_2):
@@ -31,7 +327,7 @@ def tile_obliquesoftsplitgaintable_x2_kernel(tc, x, p_words, p_scales, b, w, g, 
         four = ctx.enter_context(tc.tile_pool(name="four", bufs=4))
         three = ctx.enter_context(tc.tile_pool(name="three", bufs=3))
         two = ctx.enter_context(tc.tile_pool(name="two", bufs=2))
-        ps3 = ctx.enter_context(tc.psum_pool(name="ps3", bufs=3))
+        ps3 = ctx.enter_context(tc.psum_pool(name="ps3", bufs=2))
         ps1 = ctx.enter_context(tc.psum_pool(name="ps1", bufs=1))
         ctx.enter_context(tc.manual_schedule())
 
@@ -70,14 +366,15 @@ def tile_obliquesoftsplitgaintable_x2_kernel(tc, x, p_words, p_scales, b, w, g, 
         ident_b = keep.tile([P, P], BF16, name="ident_b", align_bytes=64)
         make_identity(nc, ident_f[:])
         make_identity(nc, ident_b[:])
-        neg_half = keep.tile([P, 1], F32, name="neg_half")
+        ones_b = keep.tile([P, P], BF16, name="ones_b", align_bytes=64)
+        nc.vector.memset(ones_b[:], 1.0)
 
         xc = [keep.tile([P, 512], U32, name="xc%d" % G, align_bytes=64) for G in range(NG)]
         xs = [keep.tile([P, 512], U8, name="xs%d" % G, align_bytes=64) for G in range(NG)]
         gc = [keep.tile([P, T], U32, name="gc%d" % G, align_bytes=64) for G in range(NG)]
         gs = [keep.tile([P, T], U8, name="gs%d" % G, align_bytes=64) for G in range(NG)]
-        h_bc = keep.tile([P, NG, 512], BF16, name="h_bc", align_bytes=64)
-        ht4 = keep.tile([P, NG], F32, name="ht4")
+        w_bc = keep.tile([P, NG, 512], BF16, name="w_bc", align_bytes=64)
+        h_ps = [ps1.tile([P, 2, 512], BF16, name="h_ps%d" % a) for a in range(2)]
         gt_sb = keep.tile([P, T], F32, name="gt_sb", align_bytes=64)
         ngt2 = keep.tile([P, T], F32, name="ngt2", align_bytes=64)
         b_half = keep.tile([P, MT], F32, name="b_half")
@@ -95,17 +392,14 @@ def tile_obliquesoftsplitgaintable_x2_kernel(tc, x, p_words, p_scales, b, w, g, 
                 banks.append(bank)
             return banks
 
-        def evac_x(G, banks, engines):
-            xg = three.tile([P, 2048], BF16, name="xg", align_bytes=64)
-            pairs = xg[:].bitcast(F32).rearrange("p (c u) -> p c u", u=2)
-            for a in range(2):
-                dst = pairs[:, 256 * a : 256 * (a + 1), :].rearrange("p (j r) u -> p j r u", j=2)
-                src = banks[a][:].rearrange("p j u r -> p j r u")
-                if engines[a] == "v":
-                    nc.vector.tensor_copy(out=dst, in_=src)
-                else:
-                    nc.scalar.copy(out=dst, in_=src)
-            return xg
+        def evac_x(G, a, engine):
+            pairs = xg_t[G][:].bitcast(F32).rearrange("p (c u) -> p c u", u=2)
+            dst = pairs[:, 256 * a : 256 * (a + 1), :].rearrange("p (r j) u -> p r j u", j=2)
+            src = bank_t[G][a][:].rearrange("p j u r -> p r j u")
+            if engine == "v":
+                nc.vector.tensor_copy(out=dst, in_=src)
+            else:
+                nc.scalar.copy(out=dst, in_=src)
 
         def quant_x(G, xg):
             nc.vector.quantize_mx(out=xc[G][:].bitcast(FP8X4), scales=xs[G][:], in_=xg[:])
@@ -113,12 +407,26 @@ def tile_obliquesoftsplitgaintable_x2_kernel(tc, x, p_words, p_scales, b, w, g, 
         b_ps = ps1.tile([P, P], BF16, name="pl")
         nc.tensor.transpose(b_ps[:], b_rows[:], ident_b[:])
         nc.vector.tensor_scalar(out=b_half[:], in0=b_ps[:, 0:MT], scalar1=0.5, scalar2=0.0, op0=ALU.mult, op1=ALU.add)
+        ht_ps = ps1.tile([P, NG * 4], F32, name="pl")
+        nc.tensor.matmul(out=ht_ps[:], lhsT=ones_b[:], rhs=h_sb[:].rearrange("p g j -> p (g j)"), start=True, stop=True)
 
         def h_spread(G):
-            hb = ps3.tile([P, 4, P], F32, name="hb", tag="tb")
             for j in range(4):
-                nc.tensor.matmul(out=hb[:, j, :], lhsT=h_sb[:, G, j : j + 1].to_broadcast([P, P]), rhs=ident_b[:], start=True, stop=True)
-            nc.scalar.activation(out=h_bc[:, G, :], in_=hb[:].rearrange("p j n -> p (j n)"), func=ACT.Copy, accum_out=ht4[:, G : G + 1])
+                c = 256 * (G % 2) + 128 * (j // 2)
+                nc.tensor.matmul(
+                    out=h_ps[G // 2][:, j % 2, c : c + P], lhsT=h_sb[:, G, j : j + 1].to_broadcast([P, P]), rhs=ident_b[:], start=True, stop=True
+                )
+
+        wb_t = {}
+
+        def w_spread(G):
+            wb = ps3.tile([P, 2, 2, P], F32, name="wb", tag="tb")
+            for j in range(4):
+                nc.tensor.matmul(out=wb[:, j // 2, j % 2, :], lhsT=w_sb[:, G, j : j + 1].to_broadcast([P, P]), rhs=ident_b[:], start=True, stop=True)
+            wb_t[G] = wb
+
+        def w_evac(G):
+            nc.scalar.copy(out=w_bc[:, G, :].rearrange("p (u n e) -> p u n e", u=2, e=2), in_=wb_t[G][:].rearrange("p u e n -> p u n e"))
 
         ht = keep.tile([P, 1], F32, name="ht")
         ssum = keep.tile([P, 1], F32, name="ssum")
@@ -131,7 +439,9 @@ def tile_obliquesoftsplitgaintable_x2_kernel(tc, x, p_words, p_scales, b, w, g, 
         neg_c = keep.tile([P, 1], F32, name="neg_c")
 
         def head_constants_1():
-            nc.vector.reduce_sum(out=ht[:], in_=ht4[:], axis=AX.X)
+            nc.vector.reduce_sum(out=ht[:], in_=ht_ps[:], axis=AX.X)
+
+        def head_constants_1g():
             nc.gpsimd.tensor_scalar(out=ssum[:], in0=ht[:], scalar1=1.0, scalar2=2.0 * LAM, op0=ALU.mult, op1=ALU.add)
             nc.gpsimd.tensor_scalar(out=two_s[:], in0=ssum[:], scalar1=2.0, scalar2=0.0, op0=ALU.mult, op1=ALU.add)
             nc.gpsimd.tensor_scalar(out=c_den[:], in0=ht[:], scalar1=LAM, scalar2=ssum[:], op0=ALU.add, op1=ALU.mult)
@@ -139,12 +449,17 @@ def tile_obliquesoftsplitgaintable_x2_kernel(tc, x, p_words, p_scales, b, w, g, 
         def head_constants_2():
             nc.vector.reciprocal(out=r_s[:], in_=ssum[:])
             nc.vector.reciprocal(out=c_rec[:], in_=c_den[:])
+
+        def head_constants_2g():
             nc.gpsimd.tensor_scalar(out=nr_s[:], in0=r_s[:], scalar1=-1.0, scalar2=0.0, op0=ALU.mult, op1=ALU.add)
             nc.gpsimd.tensor_scalar(out=n2r_s[:], in0=r_s[:], scalar1=-2.0, scalar2=0.0, op0=ALU.mult, op1=ALU.add)
             nc.gpsimd.tensor_scalar(out=neg_c[:], in0=c_rec[:], scalar1=-0.5 * LAM, scalar2=0.0, op0=ALU.mult, op1=ALU.add)
 
-        s_t, q_t, hdp_t, tb_t, d_t, v_t, sq_t, r_t, rb_t, pb_t, pg_t, prod_t, z_t = ({} for k in range(13))
+        s_t, q_t, hdp_t, tb_t, d_t, v_t, sq_t, r_t, rb_t, pb_t, pg_t, tw_t, qn_t, z_t = ({} for k in range(14))
         qc_t, qs_t, hs_t, den_t, k_t = ({} for k in range(5))
+
+        def gset(i):
+            return GSET.get(i, GSET[-1])
 
         def live(i):
             return 0 <= i < MT
@@ -152,10 +467,10 @@ def tile_obliquesoftsplitgaintable_x2_kernel(tc, x, p_words, p_scales, b, w, g, 
         def z_step(i, G):
             if not live(i):
                 return
-            if G == 0:
+            if i not in s_t:
                 s_t[i] = three.tile([P, NG, 512], F32, name="s", align_bytes=64)
-                q_t[i] = two.tile([P, NG, P, 4], BF16, name="q", align_bytes=64)
-                hdp_t[i] = three.tile([P, NG], F32, name="hdp")
+                q_t[i] = four.tile([P, NG, P, 4], BF16, name="q", align_bytes=64)
+                hdp_t[i] = four.tile([P, 2], F32, name="hdp")
             zb = ps3.tile([P, 512], F32, name="zb", tag="zb")
             nc.tensor.matmul_mx(
                 out=zb[:],
@@ -174,15 +489,16 @@ def tile_obliquesoftsplitgaintable_x2_kernel(tc, x, p_words, p_scales, b, w, g, 
             nc.scalar.activation(out=s_t[i][:, G, :], in_=z_t[i, G][:], func=ACT.Tanh, bias=b_half[:, i : i + 1], scale=0.5)
 
         def t_step(i, G):
-            if not live(i):
+            if not live(i) or G in gset(i):
                 return
             tb = ps3.tile([P, 4, P], F32, name="tb", tag="tb")
             for j in range(4):
-                nc.tensor.transpose(tb[:, j, :], s_t[i][:, G, P * j : P * (j + 1)], ident_f[:])
+                c = 256 * (j // 2)
+                nc.tensor.transpose(tb[:, j, :], s_t[i][:, G, c + j % 2 : c + 256 : 2], ident_f[:])
             tb_t[i, G] = tb
 
         def evac(i, G):
-            if not live(i):
+            if not live(i) or G in gset(i):
                 return
             nc.vector.tensor_tensor(
                 out=q_t[i][:, G, :, :],
@@ -191,37 +507,57 @@ def tile_obliquesoftsplitgaintable_x2_kernel(tc, x, p_words, p_scales, b, w, g, 
                 op=ALU.mult,
             )
 
-        def hd_v(i, G):
-            if not live(i) or G not in HD_ON_V:
+        def g_mul(i, G):
+            if not live(i) or G not in gset(i):
                 return
-            junk = two.tile([P, 512], F32, name="junk", align_bytes=64)
+            qn_t[i, G] = four.tile([P, 512], BF16, name="qn", align_bytes=64, bufs=6)
+            nc.gpsimd.tensor_tensor(out=qn_t[i, G][:], in0=s_t[i][:, G, :], in1=w_bc[:, G, :], op=ALU.mult)
+
+        def tw_step(i, Gs):
+            Gs = [G for G in Gs if live(i) and G in gset(i)]
+            if not Gs:
+                return
+            tb = ps3.tile([P, 2, 2, P], F32, name="tw", tag="tb")
+            for k, G in enumerate(Gs):
+                words = qn_t[i, G][:].bitcast(F32)
+                for u in range(2):
+                    nc.tensor.transpose(tb[:, k, u, :], words[:, P * u : P * (u + 1)], ident_f[:])
+            tw_t[i, Gs[0]] = tb
+
+        def evw(i, Gs, engine="s"):
+            Gs = [G for G in Gs if live(i) and G in gset(i)]
+            if not Gs:
+                return
+            n = len(Gs)
+            dst = q_t[i][:].rearrange("p g m j -> p (g m j)").bitcast(F32).rearrange("p (g m u) -> p g m u", g=NG, u=2)[:, Gs[0] : Gs[0] + n, :, :]
+            src = tw_t[i, Gs[0]][:, 0:n, :, :].rearrange("p g u m -> p g m u")
+            if engine == "s":
+                nc.scalar.copy(out=dst, in_=src)
+            else:
+                nc.vector.tensor_copy(out=dst, in_=src)
+
+        def hd(i, a):
+            if not live(i):
+                return
+            junk = two.tile([P, 512, 2], F32, name="junk", align_bytes=64)
             nc.vector.scalar_tensor_tensor(
-                out=junk[:], in0=s_t[i][:, G, :], scalar=1.0, in1=h_bc[:, G, :], op0=ALU.mult, op1=ALU.mult, accum_out=hdp_t[i][:, G : G + 1]
+                out=junk[:],
+                in0=s_t[i][:, 2 * a : 2 * a + 2, :].rearrange("p g (q e) -> p (g q) e", e=2),
+                scalar=1.0,
+                in1=h_ps[a][:].rearrange("p e q -> p q e"),
+                op0=ALU.mult,
+                op1=ALU.mult,
+                accum_out=hdp_t[i][:, a : a + 1],
             )
-
-        def prod(i, G):
-            if not live(i) or G in HD_ON_V:
-                return
-            pr = three.tile([P, 512], F32, name="prod", align_bytes=64)
-            nc.gpsimd.tensor_tensor(out=pr[:], in0=s_t[i][:, G, :], in1=h_bc[:, G, :], op=ALU.mult)
-            prod_t[i, G] = pr
-
-        def acc(i, G):
-            if not live(i) or G in HD_ON_V:
-                return
-            junk2 = two.tile([P, 512], BF16, name="junk2", align_bytes=64)
-            nc.scalar.activation(out=junk2[:], in_=prod_t[i, G][:], func=ACT.Copy, accum_out=hdp_t[i][:, G : G + 1])
 
         def chain(i):
             if not live(i):
                 return
-            hd2 = two.tile([P, 2], F32, name="hd2")
-            hd1 = two.tile([P, 1], F32, name="hd1")
-            hq = two.tile([P, 1], F32, name="hq")
-            hs_t[i] = two.tile([P, 1], F32, name="hs")
-            den_t[i] = two.tile([P, 1], F32, name="den")
-            nc.gpsimd.tensor_tensor(out=hd2[:], in0=hdp_t[i][:, 0:2], in1=hdp_t[i][:, 2:4], op=ALU.add)
-            nc.gpsimd.tensor_tensor(out=hd1[:], in0=hd2[:, 0:1], in1=hd2[:, 1:2], op=ALU.add)
+            hd1 = four.tile([P, 1], F32, name="hd1")
+            hq = four.tile([P, 1], F32, name="hq")
+            hs_t[i] = four.tile([P, 1], F32, name="hs")
+            den_t[i] = four.tile([P, 1], F32, name="den")
+            nc.gpsimd.tensor_tensor(out=hd1[:], in0=hdp_t[i][:, 0:1], in1=hdp_t[i][:, 1:2], op=ALU.add)
             nc.gpsimd.tensor_scalar(out=hs_t[i][:], in0=hd1[:], scalar1=nr_s[:], scalar2=0.0, op0=ALU.mult, op1=ALU.add)
             nc.gpsimd.tensor_tensor(out=hq[:], in0=hd1[:], in1=hd1[:], op=ALU.mult)
             nc.gpsimd.tensor_scalar(out=den_t[i][:], in0=hq[:], scalar1=n2r_s[:], scalar2=two_s[:], op0=ALU.mult, op1=ALU.add)
@@ -229,28 +565,24 @@ def tile_obliquesoftsplitgaintable_x2_kernel(tc, x, p_words, p_scales, b, w, g, 
         def recip(i):
             if not live(i):
                 return
-            k_t[i] = two.tile([P, 1], F32, name="kk")
+            k_t[i] = four.tile([P, 1], F32, name="kk")
             nc.vector.reciprocal(out=k_t[i][:], in_=den_t[i][:])
 
         def quant_q(i):
             if not live(i):
                 return
-            qc_t[i] = two.tile([P, NG, P], U32, name="qc", align_bytes=64)
-            qs_t[i] = two.tile([P, NG, P], U8, name="qs", align_bytes=64)
+            qc_t[i] = four.tile([P, NG, P], U32, name="qc", align_bytes=64)
+            qs_t[i] = four.tile([P, NG, P], U8, name="qs", align_bytes=64)
             nc.vector.quantize_mx(
                 out=qc_t[i][:].rearrange("p g m -> p (g m)").bitcast(FP8X4),
                 scales=qs_t[i][:].rearrange("p g m -> p (g m)"),
                 in_=q_t[i][:].rearrange("p g m j -> p (g m j)"),
             )
 
-        def d_step(i):
-            if not live(i):
-                return
-            if i < MT - 1:
+        def d_step(i, half):
+            if half == 0:
                 d_t[i] = ps1.tile([P, T], F32, name="db")
-            else:
-                d_t[i] = ps3.tile([P, T], F32, name="d_last", tag="zb")
-            for G in range(NG):
+            for G in (2 * half, 2 * half + 1):
                 nc.tensor.matmul_mx(
                     out=d_t[i][:],
                     lhsT=qc_t[i][:, G, :].bitcast(FP8X4),
@@ -264,26 +596,26 @@ def tile_obliquesoftsplitgaintable_x2_kernel(tc, x, p_words, p_scales, b, w, g, 
         def v_step(i):
             if not live(i):
                 return
-            v_t[i] = two.tile([P, T], F32, name="v", align_bytes=64)
+            v_t[i] = four.tile([P, T], F32, name="v", align_bytes=64)
             nc.vector.scalar_tensor_tensor(out=v_t[i][:], in0=gt_sb[:], scalar=hs_t[i][:], in1=d_t[i][:], op0=ALU.mult, op1=ALU.add)
 
         def sq_step(i):
             if not live(i):
                 return
-            sq_t[i] = two.tile([P, T], F32, name="sq", align_bytes=64)
+            sq_t[i] = four.tile([P, T], F32, name="sq", align_bytes=64)
             nc.scalar.activation(out=sq_t[i][:], in_=v_t[i][:], func=ACT.Square)
 
         def r_step(i):
             if not live(i):
                 return
-            r_t[i] = two.tile([P, T], F32, name="r", align_bytes=64)
+            r_t[i] = four.tile([P, T], F32, name="r", align_bytes=64)
             nc.vector.scalar_tensor_tensor(out=r_t[i][:], in0=sq_t[i][:], scalar=k_t[i][:], in1=ngt2[:], op0=ALU.mult, op1=ALU.add)
             nc.sync.dma_start(out=out_0[P * i : P * (i + 1), :], in_=r_t[i][:])
 
         def rb_step(i):
             if not live(i):
                 return
-            rb_t[i] = two.tile([P, T], BF16, name="rb", align_bytes=64)
+            rb_t[i] = four.tile([P, T], BF16, name="rb", align_bytes=64)
             nc.scalar.copy(out=rb_t[i][:], in_=r_t[i][:])
 
         def p_step(i):
@@ -298,7 +630,7 @@ def tile_obliquesoftsplitgaintable_x2_kernel(tc, x, p_words, p_scales, b, w, g, 
         def pg_step(i):
             if not live(i):
                 return
-            pg_t[i] = two.tile([P, 4 * P], BF16, name="pg", align_bytes=64)
+            pg_t[i] = four.tile([P, 4 * P], BF16, name="pg", align_bytes=64)
             nc.scalar.copy(out=pg_t[i][:].bitcast(F32).rearrange("p (m u) -> p m u", u=2), in_=pb_t[i][:].rearrange("p u m -> p m u"))
 
         def qp_step(i):
@@ -317,7 +649,8 @@ def tile_obliquesoftsplitgaintable_x2_kernel(tc, x, p_words, p_scales, b, w, g, 
 
         gg_t = {}
 
-        def ig(G, engine):
+        def ig(G):
+            engine = IG[G]
             gg_t[G] = four.tile([P, T, 4], BF16, name="gg", align_bytes=64)
             src = g_raw[G][:].rearrange("p j t -> p t j")
             if engine == "g":
@@ -336,111 +669,50 @@ def tile_obliquesoftsplitgaintable_x2_kernel(tc, x, p_words, p_scales, b, w, g, 
                     out=bank[:], lhsT=w_sb[:, G, j : j + 1].to_broadcast([P, P]), rhs=g_raw[G][:, j, :], start=(G == 0 and j == 0), stop=(G == NG - 1 and j == 3)
                 )
 
-        bk0 = transpose_x(0)
-        xg0 = evac_x(0, bk0, "vs")
-        bk1 = transpose_x(1)
-        quant_x(0, xg0)
-        xg1 = evac_x(1, bk1, "vs")
-        z_step(0, 0)
-        tanh(0, 0)
-        h_spread(0)
-        h_spread(1)
-        quant_x(1, xg1)
-        bk2 = transpose_x(2)
-        xg2 = evac_x(2, bk2, "vs")
-        z_step(0, 1)
-        tanh(0, 1)
-        ig(0, "g")
-        t_step(0, 0)
-        quant_x(2, xg2)
-        evac(0, 0)
-        bk3 = transpose_x(3)
-        xg3 = evac_x(3, bk3, "vs")
-        z_step(0, 2)
-        tanh(0, 2)
-        quant_x(3, xg3)
-        t_step(0, 1)
-        h_spread(2)
-        h_spread(3)
-        z_step(0, 3)
-        tanh(0, 3)
-        head_constants_1()
-        ig(1, "g")
+        plan = []
 
-        for i in range(1, MT + 3):
-            z_step(i, 0)
-            tanh(i, 0)
-            z_step(i, 1)
-            tanh(i, 1)
-            if i == 1:
-                ig(2, "g")
-                ig(3, "s")
-                prod(0, 1)
-            if i != MT + 1:
-                chain(i - 2)
-            prod(i - 1, 3)
-            if i < MT:
-                d_step(i - 2)
-            evac(i - 1, 1)
-            hd_v(i - 1, 0)
-            if i != MT:
-                v_step(i - 2)
-                sq_step(i - 2)
-            t_step(i - 1, 2)
-            evac(i - 1, 2)
-            recip(i - 2)
-            if i < MT:
-                hd_v(i - 1, 2)
-            t_step(i - 1, 3)
-            evac(i - 1, 3)
-            if i == MT:
-                hd_v(i - 1, 2)
-            p_step(i - 3)
-            pg_step(i - 3)
-            if i == 1:
-                gt_bank = ps1.tile([P, T], F32, name="pl")
-                gt_step(0, gt_bank)
-                gq(0)
-                gt_step(1, gt_bank)
-            if i > 1:
-                acc(i - 1, 1)
-            if i == 2:
-                nc.vector.scalar_tensor_tensor(out=ngt2[:], in0=gt_bank[:], scalar=neg_c[:], in1=gt_sb[:], op0=ALU.mult, op1=ALU.mult)
-            if i < MT:
-                r_step(i - 2)
-                quant_q(i - 1)
-            elif i == MT:
-                acc(i - 1, 3)
-                chain(i - 1)
-                quant_q(i - 1)
-                d_step(i - 2)
-                v_step(i - 2)
-                sq_step(i - 2)
-                d_step(i - 1)
-                r_step(i - 2)
+        def at(time, step, *args):
+            plan.append((time, len(plan), step, args))
+
+        xg_t, bank_t, gt_bank = {}, {}, {}
+
+        def xt_step(G):
+            bank_t[G] = transpose_x(G)
+
+        def xe_step(G, a):
+            if G not in xg_t:
+                xg_t[G] = four.tile([P, 2048], BF16, name="xg", align_bytes=64)
+            evac_x(G, a, XE[G][a])
+
+        def xq_step(G):
+            quant_x(G, xg_t[G])
+
+        def gt2_step(G):
+            if G == 0:
+                gt_bank[0] = ps1.tile([P, T], F32, name="pl")
+            gt_step(G, gt_bank[0])
+
+        def gtc_step():
+            nc.scalar.copy(out=gt_sb[:], in_=gt_bank[0][:])
+
+        def ng_step():
+            nc.vector.scalar_tensor_tensor(out=ngt2[:], in0=gt_bank[0][:], scalar=neg_c[:], in1=gt_sb[:], op0=ALU.mult, op1=ALU.mult)
+
+        steps = {
+            "xt": xt_step, "xe": xe_step, "xq": xq_step, "hs": h_spread, "wp": w_spread, "we": w_evac,
+            "k1": head_constants_1, "k2": head_constants_1g, "k3": head_constants_2, "k4": head_constants_2g,
+            "ig": ig, "gq": gq, "gt": gt2_step, "gtc": gtc_step, "ng": ng_step,
+            "z": z_step, "th": tanh, "gm": g_mul, "t": t_step, "ev": evac, "hd": hd, "ch": chain, "rk": recip, "q": quant_q, "d": d_step,
+            "v": v_step, "sq": sq_step, "r": r_step, "rb": rb_step, "p": p_step, "pg": pg_step, "qp": qp_step,
+        }
+        for key, time in PLAN:
+            name, a = key[0], list(key[1:])
+            if name == "tw":
+                at(time, tw_step, a[0], a[1:])
+            elif name == "ew":
+                at(time, evw, a[0], a[1:])
             else:
-                r_step(i - 2)
-            z_step(i, 2)
-            tanh(i, 2)
-            z_step(i, 3)
-            tanh(i, 3)
-            if i == 1:
-                acc(0, 1)
-            if i != MT:
-                acc(i - 1, 3)
-            rb_step(i - 2)
-            t_step(i, 0)
-            qp_step(i - 3)
-            if i == 1:
-                gq(1)
-            evac(i, 0)
-            prod(i, 1)
-            if i == 1:
-                gq(2)
-                head_constants_2()
-                gq(3)
-            t_step(i, 1)
-            if i == 1:
-                gt_step(2, gt_bank)
-                gt_step(3, gt_bank)
-                nc.scalar.copy(out=gt_sb[:], in_=gt_bank[:])
+                at(time, steps[name], *a)
+
+        for entry in sorted(plan):
+            entry[2](*entry[3])

from contextlib import ExitStack

import concourse.mybir as mybir
from concourse.masks import make_identity

N, D, M, T = 2048, 512, 1024, 512
FLOPS = 2 * N * D * M + 2 * N * M * T

F32 = mybir.dt.float32
BF16 = mybir.dt.bfloat16
U32 = mybir.dt.uint32
I32 = mybir.dt.int32
U8 = mybir.dt.uint8
FP8X4 = mybir.dt.float8_e4m3fn_x4
FP4X4 = mybir.dt.float4_e2m1fn_x4
ACT = mybir.ActivationFunctionType
ALU = mybir.AluOpType
AX = mybir.AxisListType

P = 128
NG = N // 512
MT = M // P
LAM = 64.0

XE = ("vs", "vs", "vs", "vs")
IG = ("g", "s", "g", "s")
GSET = {0: (), -1: (0, 1, 2)}
PLAN = (
    (('ig', 2), 0),
    (('k1',), 1),
    (('xt', 0), 2),
    (('xe', 0, 0), 3),
    (('xe', 0, 1), 4),
    (('xq', 0), 5),
    (('xt', 1), 6),
    (('xe', 1, 0), 7),
    (('xe', 1, 1), 8),
    (('xq', 1), 9),
    (('wp', 0), 10),
    (('we', 0), 11),
    (('hs', 1), 12),
    (('wp', 2), 13),
    (('we', 2), 14),
    (('z', 0, 1), 15),
    (('th', 0, 1), 16),
    (('xt', 2), 17),
    (('xe', 2, 0), 18),
    (('xe', 2, 1), 19),
    (('xq', 2), 20),
    (('z', 0, 0), 21),
    (('th', 0, 0), 22),
    (('hs', 0), 23),
    (('xt', 3), 24),
    (('xe', 3, 0), 25),
    (('xe', 3, 1), 26),
    (('xq', 3), 27),
    (('wp', 1), 28),
    (('we', 1), 29),
    (('z', 0, 2), 30),
    (('hs', 3), 31),
    (('z', 1, 1), 32),
    (('th', 1, 1), 33),
    (('gq', 2), 34),
    (('gm', 1, 1), 35),
    (('t', 0, 1), 36),
    (('ev', 0, 1), 37),
    (('t', 0, 0), 38),
    (('ev', 0, 0), 39),
    (('hs', 2), 40),
    (('hd', 0, 0), 41),
    (('ig', 0), 42),
    (('th', 0, 2), 43),
    (('z', 0, 3), 44),
    (('th', 0, 3), 45),
    (('z', 1, 2), 46),
    (('th', 1, 2), 47),
    (('gm', 1, 2), 48),
    (('z', 1, 0), 49),
    (('th', 1, 0), 50),
    (('gm', 1, 0), 51),
    (('t', 0, 3), 52),
    (('ev', 0, 3), 53),
    (('z', 1, 3), 54),
    (('t', 0, 2), 55),
    (('hd', 0, 1), 56),
    (('ev', 0, 2), 57),
    (('gq', 0), 58),
    (('q', 0), 59),
    (('ig', 1), 60),
    (('th', 1, 3), 61),
    (('hd', 1, 0), 62),
    (('k2',), 63),
    (('k3',), 64),
    (('k4',), 65),
    (('ch', 0), 66),
    (('gt', 0), 67),
    (('gt', 1), 68),
    (('gq', 1), 69),
    (('ig', 3), 70),
    (('gq', 3), 71),
    (('t', 1, 3), 72),
    (('ev', 1, 3), 73),
    (('z', 2, 1), 74),
    (('th', 2, 1), 75),
    (('gm', 2, 1), 76),
    (('rk', 0), 77),
    (('hd', 1, 1), 78),
    (('tw', 1, 0, 1), 79),
    (('ew', 1, 0, 1), 80),
    (('z', 2, 0), 81),
    (('th', 2, 0), 82),
    (('gm', 2, 0), 83),
    (('hd', 2, 0), 84),
    (('gt', 2), 85),
    (('gt', 3), 86),
    (('gtc',), 87),
    (('z', 2, 2), 88),
    (('th', 2, 2), 89),
    (('gm', 2, 2), 90),
    (('d', 0, 0), 91),
    (('d', 0, 1), 92),
    (('v', 0), 93),
    (('ch', 1), 94),
    (('tw', 1, 2), 95),
    (('ew', 1, 2), 96),
    (('q', 1), 97),
    (('z', 2, 3), 98),
    (('th', 2, 3), 99),
    (('hd', 2, 1), 100),
    (('tw', 2, 0, 1), 101),
    (('ew', 2, 0, 1), 102),
    (('sq', 0), 103),
    (('z', 3, 0), 104),
    (('th', 3, 0), 105),
    (('gm', 3, 0), 106),
    (('rk', 1), 107),
    (('ng',), 108),
    (('r', 0), 109),
    (('tw', 2, 2), 110),
    (('ew', 2, 2), 111),
    (('t', 2, 3), 112),
    (('ev', 2, 3), 113),
    (('z', 3, 1), 114),
    (('th', 3, 1), 115),
    (('gm', 3, 1), 116),
    (('d', 1, 0), 117),
    (('d', 1, 1), 118),
    (('v', 1), 119),
    (('q', 2), 120),
    (('ch', 2), 121),
    (('z', 3, 2), 122),
    (('hd', 3, 0), 123),
    (('th', 3, 2), 124),
    (('gm', 3, 2), 125),
    (('z', 3, 3), 126),
    (('th', 3, 3), 127),
    (('hd', 3, 1), 128),
    (('rb', 0), 129),
    (('z', 4, 0), 130),
    (('th', 4, 0), 131),
    (('gm', 4, 0), 132),
    (('tw', 3, 0, 1), 133),
    (('ew', 3, 0, 1), 134),
    (('d', 2, 0), 135),
    (('t', 3, 3), 136),
    (('ev', 3, 3), 137),
    (('sq', 1), 138),
    (('r', 1), 139),
    (('d', 2, 1), 140),
    (('v', 2), 141),
    (('rk', 2), 142),
    (('tw', 3, 2), 143),
    (('ew', 3, 2), 144),
    (('p', 0), 145),
    (('pg', 0), 146),
    (('z', 4, 1), 147),
    (('th', 4, 1), 148),
    (('gm', 4, 1), 149),
    (('q', 3), 150),
    (('ch', 3), 151),
    (('z', 4, 2), 152),
    (('hd', 4, 0), 153),
    (('th', 4, 2), 154),
    (('gm', 4, 2), 155),
    (('sq', 2), 156),
    (('r', 2), 157),
    (('z', 4, 3), 158),
    (('th', 4, 3), 159),
    (('hd', 4, 1), 160),
    (('rb', 1), 161),
    (('d', 3, 0), 162),
    (('z', 5, 0), 163),
    (('th', 5, 0), 164),
    (('gm', 5, 0), 165),
    (('tw', 4, 0, 1), 166),
    (('ew', 4, 0, 1), 167),
    (('rb', 2), 168),
    (('t', 4, 3), 169),
    (('ev', 4, 3), 170),
    (('rk', 3), 171),
    (('d', 3, 1), 172),
    (('v', 3), 173),
    (('tw', 4, 2), 174),
    (('ew', 4, 2), 175),
    (('z', 5, 1), 176),
    (('th', 5, 1), 177),
    (('gm', 5, 1), 178),
    (('q', 4), 179),
    (('ch', 4), 180),
    (('z', 5, 2), 181),
    (('hd', 5, 0), 182),
    (('th', 5, 2), 183),
    (('gm', 5, 2), 184),
    (('sq', 3), 185),
    (('r', 3), 186),
    (('p', 1), 187),
    (('pg', 1), 188),
    (('z', 5, 3), 189),
    (('th', 5, 3), 190),
    (('hd', 5, 1), 191),
    (('d', 4, 0), 192),
    (('z', 6, 0), 193),
    (('th', 6, 0), 194),
    (('gm', 6, 0), 195),
    (('tw', 5, 0, 1), 196),
    (('ew', 5, 0, 1), 197),
    (('t', 5, 3), 198),
    (('ev', 5, 3), 199),
    (('rk', 4), 200),
    (('rb', 3), 201),
    (('d', 4, 1), 202),
    (('v', 4), 203),
    (('tw', 5, 2), 204),
    (('ew', 5, 2), 205),
    (('z', 6, 1), 206),
    (('th', 6, 1), 207),
    (('gm', 6, 1), 208),
    (('q', 5), 209),
    (('ch', 5), 210),
    (('z', 6, 2), 211),
    (('th', 6, 2), 212),
    (('gm', 6, 2), 213),
    (('p', 2), 214),
    (('pg', 2), 215),
    (('hd', 6, 0), 216),
    (('sq', 4), 217),
    (('r', 4), 218),
    (('z', 6, 3), 219),
    (('th', 6, 3), 220),
    (('hd', 6, 1), 221),
    (('d', 5, 0), 222),
    (('p', 3), 223),
    (('pg', 3), 224),
    (('z', 7, 0), 225),
    (('th', 7, 0), 226),
    (('gm', 7, 0), 227),
    (('tw', 6, 0, 1), 228),
    (('ew', 6, 0, 1), 229),
    (('t', 6, 3), 230),
    (('ev', 6, 3), 231),
    (('rk', 5), 232),
    (('rb', 4), 233),
    (('d', 5, 1), 234),
    (('v', 5), 235),
    (('tw', 6, 2), 236),
    (('ew', 6, 2), 237),
    (('z', 7, 1), 238),
    (('th', 7, 1), 239),
    (('gm', 7, 1), 240),
    (('qp', 0), 241),
    (('z', 7, 2), 242),
    (('q', 6), 243),
    (('qp', 1), 244),
    (('hd', 7, 0), 245),
    (('sq', 5), 246),
    (('r', 5), 247),
    (('ch', 6), 248),
    (('z', 7, 3), 249),
    (('th', 7, 2), 250),
    (('gm', 7, 2), 251),
    (('p', 4), 252),
    (('pg', 4), 253),
    (('th', 7, 3), 254),
    (('hd', 7, 1), 255),
    (('d', 6, 0), 256),
    (('tw', 7, 0, 1), 257),
    (('ew', 7, 0, 1), 258),
    (('t', 7, 3), 259),
    (('ev', 7, 3), 260),
    (('rb', 5), 261),
    (('d', 6, 1), 262),
    (('v', 6), 263),
    (('tw', 7, 2), 264),
    (('ew', 7, 2), 265),
    (('q', 7), 266),
    (('rk', 6), 267),
    (('sq', 6), 268),
    (('r', 6), 269),
    (('ch', 7), 270),
    (('qp', 2), 271),
    (('p', 5), 272),
    (('pg', 5), 273),
    (('rb', 6), 274),
    (('d', 7, 0), 275),
    (('rk', 7), 276),
    (('qp', 3), 277),
    (('d', 7, 1), 278),
    (('v', 7), 279),
    (('sq', 7), 280),
    (('r', 7), 281),
    (('p', 6), 282),
    (('pg', 6), 283),
    (('rb', 7), 284),
    (('qp', 4), 285),
    (('p', 7), 286),
    (('pg', 7), 287),
    (('qp', 5), 288),
    (('qp', 6), 289),
    (('qp', 7), 290),
)


def tile_obliquesoftsplitgaintable_x2_kernel(tc, x, p_words, p_scales, b, w, g, h, out_0, out_1, out_2):
    nc = tc.nc
    with ExitStack() as ctx:
        keep = ctx.enter_context(tc.tile_pool(name="keep", bufs=1))
        four = ctx.enter_context(tc.tile_pool(name="four", bufs=4))
        three = ctx.enter_context(tc.tile_pool(name="three", bufs=3))
        two = ctx.enter_context(tc.tile_pool(name="two", bufs=2))
        ps3 = ctx.enter_context(tc.psum_pool(name="ps3", bufs=2))
        ps1 = ctx.enter_context(tc.psum_pool(name="ps1", bufs=1))
        ctx.enter_context(tc.manual_schedule())

        x_raw, g_raw = [], []
        for G in range(NG):
            xr = four.tile([P, 4, D], BF16, name="x_raw", align_bytes=64)
            x_raw.append(xr)
        for G in range(NG):
            gr = four.tile([P, 4, T], BF16, name="g_raw", align_bytes=64)
            g_raw.append(gr)
        pw = keep.tile([P, 2 * M], U8, name="pw", align_bytes=64)
        psc = keep.tile([P, M], U8, name="psc", align_bytes=64)
        w_sb = keep.tile([P, NG, 4], BF16, name="w_sb")
        h_sb = keep.tile([P, NG, 4], BF16, name="h_sb")
        b_rows = keep.tile([P, P], BF16, name="b_rows", align_bytes=64)

        nc.vector.memset(psc[:].bitcast(I32), 0)
        nc.vector.memset(b_rows[:], 0.0)

        def load_x(G):
            nc.sync.dma_start(out=x_raw[G][:], in_=x[512 * G : 512 * (G + 1), :].rearrange("(p j) k -> p j k", j=4))

        load_x(0)
        nc.sync.dma_start(out=pw[:].bitcast(I32), in_=p_words[0].bitcast(I32))
        for G in range(1, NG):
            load_x(G)
        for G in range(NG):
            nc.sync.dma_start(out=g_raw[G][:], in_=g[512 * G : 512 * (G + 1), :].rearrange("(p j) t -> p j t", j=4))
        nc.scalar.dma_start(out=h_sb[:], in_=h.rearrange("(g p j) -> p g j", p=P, j=4))
        nc.scalar.dma_start(out=w_sb[:], in_=w.rearrange("(g p j) -> p g j", p=P, j=4))
        nc.scalar.dma_start(out=b_rows[0:MT, :], in_=b.rearrange("(i c) -> i c", c=P))
        for r in range(4):
            nc.scalar.dma_start(out=psc[r:P:32, :].bitcast(I32), in_=p_scales[0, r:16:4, :].bitcast(I32))

        ident_f = keep.tile([P, P], F32, name="ident_f", align_bytes=64)
        ident_b = keep.tile([P, P], BF16, name="ident_b", align_bytes=64)
        make_identity(nc, ident_f[:])
        make_identity(nc, ident_b[:])
        ones_b = keep.tile([P, P], BF16, name="ones_b", align_bytes=64)
        nc.vector.memset(ones_b[:], 1.0)

        xc = [keep.tile([P, 512], U32, name="xc%d" % G, align_bytes=64) for G in range(NG)]
        xs = [keep.tile([P, 512], U8, name="xs%d" % G, align_bytes=64) for G in range(NG)]
        gc = [keep.tile([P, T], U32, name="gc%d" % G, align_bytes=64) for G in range(NG)]
        gs = [keep.tile([P, T], U8, name="gs%d" % G, align_bytes=64) for G in range(NG)]
        w_bc = keep.tile([P, NG, 512], BF16, name="w_bc", align_bytes=64)
        h_ps = [ps1.tile([P, 2, 512], BF16, name="h_ps%d" % a) for a in range(2)]
        gt_sb = keep.tile([P, T], F32, name="gt_sb", align_bytes=64)
        ngt2 = keep.tile([P, T], F32, name="ngt2", align_bytes=64)
        b_half = keep.tile([P, MT], F32, name="b_half")
        oc = [keep.tile([P, 256], U32, name="oc%d" % a, align_bytes=64) for a in range(MT // 2)]
        osc = keep.tile([P, M], U8, name="osc", align_bytes=64)

        def transpose_x(G):
            words = x_raw[G][:].bitcast(F32)
            banks = []
            for a in range(2):
                bank = ps3.tile([P, 2, 2, P], F32, name="x_ps", tag="tb" if a == 0 else "zb")
                for jj in range(2):
                    for u in range(2):
                        nc.tensor.transpose(bank[:, jj, u, :], words[:, 2 * a + jj, u::2], ident_f[:])
                banks.append(bank)
            return banks

        def evac_x(G, a, engine):
            pairs = xg_t[G][:].bitcast(F32).rearrange("p (c u) -> p c u", u=2)
            dst = pairs[:, 256 * a : 256 * (a + 1), :].rearrange("p (r j) u -> p r j u", j=2)
            src = bank_t[G][a][:].rearrange("p j u r -> p r j u")
            if engine == "v":
                nc.vector.tensor_copy(out=dst, in_=src)
            else:
                nc.scalar.copy(out=dst, in_=src)

        def quant_x(G, xg):
            nc.vector.quantize_mx(out=xc[G][:].bitcast(FP8X4), scales=xs[G][:], in_=xg[:])

        b_ps = ps1.tile([P, P], BF16, name="pl")
        nc.tensor.transpose(b_ps[:], b_rows[:], ident_b[:])
        nc.vector.tensor_scalar(out=b_half[:], in0=b_ps[:, 0:MT], scalar1=0.5, scalar2=0.0, op0=ALU.mult, op1=ALU.add)
        ht_ps = ps1.tile([P, NG * 4], F32, name="pl")
        nc.tensor.matmul(out=ht_ps[:], lhsT=ones_b[:], rhs=h_sb[:].rearrange("p g j -> p (g j)"), start=True, stop=True)

        def h_spread(G):
            for j in range(4):
                c = 256 * (G % 2) + 128 * (j // 2)
                nc.tensor.matmul(
                    out=h_ps[G // 2][:, j % 2, c : c + P], lhsT=h_sb[:, G, j : j + 1].to_broadcast([P, P]), rhs=ident_b[:], start=True, stop=True
                )

        wb_t = {}

        def w_spread(G):
            wb = ps3.tile([P, 2, 2, P], F32, name="wb", tag="tb")
            for j in range(4):
                nc.tensor.matmul(out=wb[:, j // 2, j % 2, :], lhsT=w_sb[:, G, j : j + 1].to_broadcast([P, P]), rhs=ident_b[:], start=True, stop=True)
            wb_t[G] = wb

        def w_evac(G):
            nc.scalar.copy(out=w_bc[:, G, :].rearrange("p (u n e) -> p u n e", u=2, e=2), in_=wb_t[G][:].rearrange("p u e n -> p u n e"))

        ht = keep.tile([P, 1], F32, name="ht")
        ssum = keep.tile([P, 1], F32, name="ssum")
        two_s = keep.tile([P, 1], F32, name="two_s")
        r_s = keep.tile([P, 1], F32, name="r_s")
        nr_s = keep.tile([P, 1], F32, name="nr_s")
        n2r_s = keep.tile([P, 1], F32, name="n2r_s")
        c_den = keep.tile([P, 1], F32, name="c_den")
        c_rec = keep.tile([P, 1], F32, name="c_rec")
        neg_c = keep.tile([P, 1], F32, name="neg_c")

        def head_constants_1():
            nc.vector.reduce_sum(out=ht[:], in_=ht_ps[:], axis=AX.X)

        def head_constants_1g():
            nc.gpsimd.tensor_scalar(out=ssum[:], in0=ht[:], scalar1=1.0, scalar2=2.0 * LAM, op0=ALU.mult, op1=ALU.add)
            nc.gpsimd.tensor_scalar(out=two_s[:], in0=ssum[:], scalar1=2.0, scalar2=0.0, op0=ALU.mult, op1=ALU.add)
            nc.gpsimd.tensor_scalar(out=c_den[:], in0=ht[:], scalar1=LAM, scalar2=ssum[:], op0=ALU.add, op1=ALU.mult)

        def head_constants_2():
            nc.vector.reciprocal(out=r_s[:], in_=ssum[:])
            nc.vector.reciprocal(out=c_rec[:], in_=c_den[:])

        def head_constants_2g():
            nc.gpsimd.tensor_scalar(out=nr_s[:], in0=r_s[:], scalar1=-1.0, scalar2=0.0, op0=ALU.mult, op1=ALU.add)
            nc.gpsimd.tensor_scalar(out=n2r_s[:], in0=r_s[:], scalar1=-2.0, scalar2=0.0, op0=ALU.mult, op1=ALU.add)
            nc.gpsimd.tensor_scalar(out=neg_c[:], in0=c_rec[:], scalar1=-0.5 * LAM, scalar2=0.0, op0=ALU.mult, op1=ALU.add)

        s_t, q_t, hdp_t, tb_t, d_t, v_t, sq_t, r_t, rb_t, pb_t, pg_t, tw_t, qn_t, z_t = ({} for k in range(14))
        qc_t, qs_t, hs_t, den_t, k_t = ({} for k in range(5))

        def gset(i):
            return GSET.get(i, GSET[-1])

        def live(i):
            return 0 <= i < MT

        def z_step(i, G):
            if not live(i):
                return
            if i not in s_t:
                s_t[i] = three.tile([P, NG, 512], F32, name="s", align_bytes=64)
                q_t[i] = four.tile([P, NG, P, 4], BF16, name="q", align_bytes=64)
                hdp_t[i] = four.tile([P, 2], F32, name="hdp")
            zb = ps3.tile([P, 512], F32, name="zb", tag="zb")
            nc.tensor.matmul_mx(
                out=zb[:],
                lhsT=pw[:, 256 * i : 256 * (i + 1)].bitcast(FP4X4),
                lhsT_scale=psc[:, P * i : P * (i + 1)],
                rhs=xc[G][:].bitcast(FP8X4),
                rhs_scale=xs[G][:],
                start=True,
                stop=True,
            )
            z_t[i, G] = zb

        def tanh(i, G):
            if not live(i):
                return
            nc.scalar.activation(out=s_t[i][:, G, :], in_=z_t[i, G][:], func=ACT.Tanh, bias=b_half[:, i : i + 1], scale=0.5)

        def t_step(i, G):
            if not live(i) or G in gset(i):
                return
            tb = ps3.tile([P, 4, P], F32, name="tb", tag="tb")
            for j in range(4):
                c = 256 * (j // 2)
                nc.tensor.transpose(tb[:, j, :], s_t[i][:, G, c + j % 2 : c + 256 : 2], ident_f[:])
            tb_t[i, G] = tb

        def evac(i, G):
            if not live(i) or G in gset(i):
                return
            nc.vector.tensor_tensor(
                out=q_t[i][:, G, :, :],
                in0=tb_t[i, G][:].rearrange("p j m -> p m j"),
                in1=w_sb[:, G, :].unsqueeze(1).to_broadcast([P, P, 4]),
                op=ALU.mult,
            )

        def g_mul(i, G):
            if not live(i) or G not in gset(i):
                return
            qn_t[i, G] = four.tile([P, 512], BF16, name="qn", align_bytes=64, bufs=6)
            nc.gpsimd.tensor_tensor(out=qn_t[i, G][:], in0=s_t[i][:, G, :], in1=w_bc[:, G, :], op=ALU.mult)

        def tw_step(i, Gs):
            Gs = [G for G in Gs if live(i) and G in gset(i)]
            if not Gs:
                return
            tb = ps3.tile([P, 2, 2, P], F32, name="tw", tag="tb")
            for k, G in enumerate(Gs):
                words = qn_t[i, G][:].bitcast(F32)
                for u in range(2):
                    nc.tensor.transpose(tb[:, k, u, :], words[:, P * u : P * (u + 1)], ident_f[:])
            tw_t[i, Gs[0]] = tb

        def evw(i, Gs, engine="s"):
            Gs = [G for G in Gs if live(i) and G in gset(i)]
            if not Gs:
                return
            n = len(Gs)
            dst = q_t[i][:].rearrange("p g m j -> p (g m j)").bitcast(F32).rearrange("p (g m u) -> p g m u", g=NG, u=2)[:, Gs[0] : Gs[0] + n, :, :]
            src = tw_t[i, Gs[0]][:, 0:n, :, :].rearrange("p g u m -> p g m u")
            if engine == "s":
                nc.scalar.copy(out=dst, in_=src)
            else:
                nc.vector.tensor_copy(out=dst, in_=src)

        def hd(i, a):
            if not live(i):
                return
            junk = two.tile([P, 512, 2], F32, name="junk", align_bytes=64)
            nc.vector.scalar_tensor_tensor(
                out=junk[:],
                in0=s_t[i][:, 2 * a : 2 * a + 2, :].rearrange("p g (q e) -> p (g q) e", e=2),
                scalar=1.0,
                in1=h_ps[a][:].rearrange("p e q -> p q e"),
                op0=ALU.mult,
                op1=ALU.mult,
                accum_out=hdp_t[i][:, a : a + 1],
            )

        def chain(i):
            if not live(i):
                return
            hd1 = four.tile([P, 1], F32, name="hd1")
            hq = four.tile([P, 1], F32, name="hq")
            hs_t[i] = four.tile([P, 1], F32, name="hs")
            den_t[i] = four.tile([P, 1], F32, name="den")
            nc.gpsimd.tensor_tensor(out=hd1[:], in0=hdp_t[i][:, 0:1], in1=hdp_t[i][:, 1:2], op=ALU.add)
            nc.gpsimd.tensor_scalar(out=hs_t[i][:], in0=hd1[:], scalar1=nr_s[:], scalar2=0.0, op0=ALU.mult, op1=ALU.add)
            nc.gpsimd.tensor_tensor(out=hq[:], in0=hd1[:], in1=hd1[:], op=ALU.mult)
            nc.gpsimd.tensor_scalar(out=den_t[i][:], in0=hq[:], scalar1=n2r_s[:], scalar2=two_s[:], op0=ALU.mult, op1=ALU.add)

        def recip(i):
            if not live(i):
                return
            k_t[i] = four.tile([P, 1], F32, name="kk")
            nc.vector.reciprocal(out=k_t[i][:], in_=den_t[i][:])

        def quant_q(i):
            if not live(i):
                return
            qc_t[i] = four.tile([P, NG, P], U32, name="qc", align_bytes=64)
            qs_t[i] = four.tile([P, NG, P], U8, name="qs", align_bytes=64)
            nc.vector.quantize_mx(
                out=qc_t[i][:].rearrange("p g m -> p (g m)").bitcast(FP8X4),
                scales=qs_t[i][:].rearrange("p g m -> p (g m)"),
                in_=q_t[i][:].rearrange("p g m j -> p (g m j)"),
            )

        def d_step(i, half):
            if half == 0:
                d_t[i] = ps1.tile([P, T], F32, name="db")
            for G in (2 * half, 2 * half + 1):
                nc.tensor.matmul_mx(
                    out=d_t[i][:],
                    lhsT=qc_t[i][:, G, :].bitcast(FP8X4),
                    lhsT_scale=qs_t[i][:, G, :],
                    rhs=gc[G][:].bitcast(FP8X4),
                    rhs_scale=gs[G][:],
                    start=(G == 0),
                    stop=(G == NG - 1),
                )

        def v_step(i):
            if not live(i):
                return
            v_t[i] = four.tile([P, T], F32, name="v", align_bytes=64)
            nc.vector.scalar_tensor_tensor(out=v_t[i][:], in0=gt_sb[:], scalar=hs_t[i][:], in1=d_t[i][:], op0=ALU.mult, op1=ALU.add)

        def sq_step(i):
            if not live(i):
                return
            sq_t[i] = four.tile([P, T], F32, name="sq", align_bytes=64)
            nc.scalar.activation(out=sq_t[i][:], in_=v_t[i][:], func=ACT.Square)

        def r_step(i):
            if not live(i):
                return
            r_t[i] = four.tile([P, T], F32, name="r", align_bytes=64)
            nc.vector.scalar_tensor_tensor(out=r_t[i][:], in0=sq_t[i][:], scalar=k_t[i][:], in1=ngt2[:], op0=ALU.mult, op1=ALU.add)
            nc.sync.dma_start(out=out_0[P * i : P * (i + 1), :], in_=r_t[i][:])

        def rb_step(i):
            if not live(i):
                return
            rb_t[i] = four.tile([P, T], BF16, name="rb", align_bytes=64)
            nc.scalar.copy(out=rb_t[i][:], in_=r_t[i][:])

        def p_step(i):
            if not live(i):
                return
            pb = ps1.tile([P, 2, P], F32, name="pl")
            words = rb_t[i][:].bitcast(F32)
            for u in range(2):
                nc.tensor.transpose(pb[:, u, :], words[:, u::2], ident_f[:])
            pb_t[i] = pb

        def pg_step(i):
            if not live(i):
                return
            pg_t[i] = four.tile([P, 4 * P], BF16, name="pg", align_bytes=64)
            nc.scalar.copy(out=pg_t[i][:].bitcast(F32).rearrange("p (m u) -> p m u", u=2), in_=pb_t[i][:].rearrange("p u m -> p m u"))

        def qp_step(i):
            if not live(i):
                return
            o = oc[i // 2]
            c = P * (i % 2)
            nc.vector.quantize_mx(out=o[:, c : c + P].bitcast(FP8X4), scales=osc[:, P * i : P * (i + 1)], in_=pg_t[i][:])
            if i % 2 == 1:
                nc.sync.dma_start(
                    out=out_1[0].rearrange("p m t -> p (m t)")[:, 4 * P * (i - 1) : 4 * P * (i + 1)].bitcast(I32), in_=o[:].bitcast(I32)
                )
            if i == MT - 1:
                for Q in range(4):
                    nc.sync.dma_start(out=out_2[0, 4 * Q : 4 * (Q + 1), :].bitcast(I32), in_=osc[32 * Q : 32 * Q + 4, :].bitcast(I32))

        gg_t = {}

        def ig(G):
            engine = IG[G]
            gg_t[G] = four.tile([P, T, 4], BF16, name="gg", align_bytes=64)
            src = g_raw[G][:].rearrange("p j t -> p t j")
            if engine == "g":
                nc.gpsimd.tensor_scalar(out=gg_t[G][:], in0=src, scalar1=1.0, scalar2=0.0, op0=ALU.mult, op1=ALU.add)
            elif engine == "s":
                nc.scalar.copy(out=gg_t[G][:], in_=src)
            else:
                nc.vector.tensor_copy(out=gg_t[G][:], in_=src)

        def gq(G):
            nc.vector.quantize_mx(out=gc[G][:].bitcast(FP8X4), scales=gs[G][:], in_=gg_t[G][:].rearrange("p t j -> p (t j)"))

        def gt_step(G, bank):
            for j in range(4):
                nc.tensor.matmul(
                    out=bank[:], lhsT=w_sb[:, G, j : j + 1].to_broadcast([P, P]), rhs=g_raw[G][:, j, :], start=(G == 0 and j == 0), stop=(G == NG - 1 and j == 3)
                )

        plan = []

        def at(time, step, *args):
            plan.append((time, len(plan), step, args))

        xg_t, bank_t, gt_bank = {}, {}, {}

        def xt_step(G):
            bank_t[G] = transpose_x(G)

        def xe_step(G, a):
            if G not in xg_t:
                xg_t[G] = four.tile([P, 2048], BF16, name="xg", align_bytes=64)
            evac_x(G, a, XE[G][a])

        def xq_step(G):
            quant_x(G, xg_t[G])

        def gt2_step(G):
            if G == 0:
                gt_bank[0] = ps1.tile([P, T], F32, name="pl")
            gt_step(G, gt_bank[0])

        def gtc_step():
            nc.scalar.copy(out=gt_sb[:], in_=gt_bank[0][:])

        def ng_step():
            nc.vector.scalar_tensor_tensor(out=ngt2[:], in0=gt_bank[0][:], scalar=neg_c[:], in1=gt_sb[:], op0=ALU.mult, op1=ALU.mult)

        steps = {
            "xt": xt_step, "xe": xe_step, "xq": xq_step, "hs": h_spread, "wp": w_spread, "we": w_evac,
            "k1": head_constants_1, "k2": head_constants_1g, "k3": head_constants_2, "k4": head_constants_2g,
            "ig": ig, "gq": gq, "gt": gt2_step, "gtc": gtc_step, "ng": ng_step,
            "z": z_step, "th": tanh, "gm": g_mul, "t": t_step, "ev": evac, "hd": hd, "ch": chain, "rk": recip, "q": quant_q, "d": d_step,
            "v": v_step, "sq": sq_step, "r": r_step, "rb": rb_step, "p": p_step, "pg": pg_step, "qp": qp_step,
        }
        for key, time in PLAN:
            name, a = key[0], list(key[1:])
            if name == "tw":
                at(time, tw_step, a[0], a[1:])
            elif name == "ew":
                at(time, evw, a[0], a[1:])
            else:
                at(time, steps[name], *a)

        for entry in sorted(plan):
            entry[2](*entry[3])
